import numpy as np
import ml_dtypes


def mxq(x, axis, fmt="e4m3"):
    dtype, down = {"e4m3": (ml_dtypes.float8_e4m3fn, 7), "e5m2": (ml_dtypes.float8_e5m2, 14)}[fmt]
    v = np.moveaxis(np.asarray(x, np.float32).astype(ml_dtypes.bfloat16).astype(np.float64), axis, -1)
    blocks = v.reshape(v.shape[:-1] + (-1, 32))
    amax = np.abs(blocks).max(-1, keepdims=True)
    byte = np.maximum(np.where(amax > 0, np.frexp(amax)[1] - 1 + 127, 0) - down, 1)
    scale = np.exp2(byte - 127.0)
    codes = (blocks / scale).astype(np.float32).astype(dtype).astype(np.float64)
    return np.moveaxis((codes * scale).reshape(v.shape), -1, axis)


WIDE = False


def mx_kscale(k):
    if not WIDE:
        return np.ones(k)
    levels = np.array([10, -10, 5, -5, 0])
    if k % 512:
        return np.exp2(np.random.permutation(np.resize(levels, k // 32))).repeat(32)
    a = np.empty((k // 512, 16))
    for p in range(k // 512):
        a[p, :8] = np.random.permutation(np.resize(levels, 8))
        for g in range(8):
            far = levels[np.abs(levels - a[p, g]) >= 10]
            a[p, g + 8] = far[np.random.randint(len(far))]
    return np.exp2(a.ravel()).repeat(32)


def f64(x):
    return np.asarray(x).astype(np.float64)


def striped(idx):
    return np.tile(idx.reshape(-1, 16).T, (8, 1)).astype(np.uint16)


def unstriped(offs):
    return offs[:16].T.reshape(-1).astype(np.int64)


def pack_weight(w):
    k, n = w.shape
    w = f64(np.asarray(w, np.float32).astype(ml_dtypes.bfloat16)).reshape(k // 32, 32, n)
    amax = np.abs(w).max(1)
    byte = np.clip(np.where(amax > 0, np.frexp(amax)[1] - 1 + 127 - 7, 1), 1, 254)
    scaled = (w * np.exp2(127.0 - byte)[:, None, :]).reshape(k, n).astype(np.float32)
    words = np.ascontiguousarray(scaled.reshape(k // 512, 128, 4, n).transpose(0, 1, 3, 2)).astype(ml_dtypes.float8_e4m3fn).view(np.uint8)
    return words, np.ascontiguousarray(byte.astype(np.uint8).reshape(k // 512, 16, n))


def unpack_weight(words, scales):
    g, p, n, _ = words.shape
    vals = np.ascontiguousarray(words).view(ml_dtypes.float8_e4m3fn).astype(np.float64) * np.repeat(np.exp2(scales.astype(np.float64) - 127.0), 8, axis=1)[..., None]
    return vals.transpose(0, 1, 3, 2).reshape(g * 512, n)


E2M1 = np.array([0.0, 0.5, 1.0, 1.5, 2.0, 3.0, 4.0, 6.0, -0.0, -0.5, -1.0, -1.5, -2.0, -3.0, -4.0, -6.0])


def pack_fp4(w):
    k, n = w.shape
    w = f64(np.asarray(w, np.float32).astype(ml_dtypes.bfloat16)).reshape(k // 32, 32, n)
    amax = np.abs(w).max(1)
    mant, ex = np.frexp(amax / 6.0)
    byte = np.clip(np.where(amax > 0, np.where(mant > 0.5, ex, ex - 1) + 127, 1), 1, 254)
    scaled = (w * np.exp2(127.0 - byte)[:, None, :]).reshape(k, n).astype(np.float32)
    c = np.ascontiguousarray(scaled.reshape(k // 512, 128, 4, n).transpose(0, 1, 3, 2)).astype(ml_dtypes.float4_e2m1fn).view(np.uint8) & 0xF
    words = (c[..., 0::2] | (c[..., 1::2] << 4)).reshape(k // 512, 128, 2 * n)
    return np.ascontiguousarray(words), np.ascontiguousarray(byte.astype(np.uint8).reshape(k // 512, 16, n))


def unpack_fp4(words, scales):
    g, _, n = scales.shape
    words = np.ascontiguousarray(words).reshape(g, 128, n, 2)
    nib = np.empty((g, 128, n, 4), np.uint8)
    nib[..., 0::2] = words & 0xF
    nib[..., 1::2] = words >> 4
    vals = E2M1[nib] * np.repeat(np.exp2(scales.astype(np.float64) - 127.0), 8, axis=1)[..., None]
    return vals.transpose(0, 1, 3, 2).reshape(g * 512, n)


def planes(y):
    n, m = y.shape
    v = y.astype(np.float32).astype(ml_dtypes.bfloat16).astype(np.float64).reshape(n // 32, 32, m)
    top = np.abs(v).max(1)
    byte = np.clip(np.where(top > 0, np.frexp(top)[1] - 1 + 127 - 7, 1), 1, 254)
    codes = (v * np.exp2(127.0 - byte)[:, None, :]).reshape(n, m).astype(np.float32).astype(ml_dtypes.float8_e4m3fn).view(np.uint8)
    words = codes.reshape(n // 512, 128, 4, m).transpose(0, 1, 3, 2)
    return np.ascontiguousarray(words), np.ascontiguousarray(byte.astype(np.uint8).reshape(n // 512, 16, m))


K, T, S, N, H = 1024, 2048, 512, 512, 512


def setup_inputs():
    n = np.random.standard_normal
    s = mx_kscale(K)[:, None]
    u = mx_kscale(H)
    packed_xT = pack_weight(n((K, T)) * s)
    packed_w1 = pack_fp4(n((K, N)) / np.sqrt(K) / s)
    packed_w2 = pack_fp4(n((K, N)) / np.sqrt(K) / s)
    packed_w3 = pack_fp4(n((H, N)) / np.sqrt(H) / u[:, None])
    return {
        "x_words": packed_xT[0],
        "x_scales": packed_xT[1],
        "w1_words": packed_w1[0],
        "w1_scales": packed_w1[1],
        "w2_words": packed_w2[0],
        "w2_scales": packed_w2[1],
        "unit": (np.random.uniform(0.6, 1.4, (H, 1)) * u[:, None]).astype(np.float32),
        "w3_words": packed_w3[0],
        "w3_scales": packed_w3[1],
        "offs": striped(np.random.permutation(T)[:S]),
        "cle": striped(np.random.permutation(S)),
    }


def reference(x_words, x_scales, w1_words, w1_scales, w2_words, w2_scales, unit, w3_words, w3_scales, offs, cle):
    xq = unpack_weight(x_words, x_scales)[:, unstriped(offs)]
    y = unpack_fp4(w1_words, w1_scales).T @ xq
    z1 = unpack_fp4(w2_words, w2_scales).T @ xq
    zc = z1[:, unstriped(cle)]
    sum_ = y * zc
    s1 = sum_[:, unstriped(cle)]
    hid = f64(unit) * np.maximum(sum_, s1)
    out_0 = unpack_fp4(w3_words, w3_scales).T @ mxq(hid, 0, "e4m3")
    return (out_0,) + planes(out_0)

@@ -1,0 +1,217 @@
+from contextlib import ExitStack
+
+import concourse.mybir as mybir
+
+K, T, S, H, N = 1024, 2048, 512, 512, 512
+FLOPS = 2 * K * S * H * 2 + 2 * H * S * N
+
+F32 = mybir.dt.float32
+BF16 = mybir.dt.bfloat16
+I32 = mybir.dt.int32
+U32 = mybir.dt.uint32
+U16 = mybir.dt.uint16
+U8 = mybir.dt.uint8
+FP8X4 = mybir.dt.float8_e4m3fn_x4
+FP4X4 = mybir.dt.float4_e2m1fn_x4
+ALU = mybir.AluOpType
+COPY = mybir.ActivationFunctionType.Copy
+
+P = 128
+PACK = 4
+PASSES = K // (P * PACK)
+QUADS = 4
+HALF = S // 2
+CHUNKS = (256, 128, 128)
+VECTOR_GATHERS = ((1, 0), (1, 1), (3, 1))
+
+
+def tile_picked_ycallgr_max_po_kernel(
+    tc, x_words, x_scales, w1_words, w1_scales, w2_words, w2_scales, unit, w3_words, w3_scales, offs, cle,
+    out_0, out_1, out_2,
+):
+    nc = tc.nc
+    with ExitStack() as ctx:
+        lists = ctx.enter_context(tc.tile_pool(name="lists", bufs=1))
+        keep = ctx.enter_context(tc.tile_pool(name="keep", bufs=1))
+        psum = ctx.enter_context(tc.psum_pool(name="psum", bufs=1))
+
+        offs_sb = lists.tile([P, S // 16], U16, name="offs_sb")
+        cle_sb = lists.tile([P, S // 16], U16, name="cle_sb")
+        x_tab = [keep.tile([P, T], I32, name=f"x_tab{o}") for o in range(PASSES)]
+        xs_tab = keep.tile([P, T], U8, name="xs_tab")
+        w_raw = keep.tile([P, PASSES, 2 * H], U8, name="w_raw")
+        ws_raw = keep.tile([P, PASSES, H], U8, name="ws_raw")
+        unit_sb = keep.tile([P, PACK], F32, name="unit_sb")
+
+        def load_scale_rows(queues, tile, scales):
+            passes = scales.shape[0]
+            for q in range(QUADS):
+                queues[q].dma_start(
+                    out=tile[32 * q : 32 * q + 4, 0:passes, :].bitcast(I32),
+                    in_=scales[:, 4 * q : 4 * q + 4, :].rearrange("o r c -> r o c").bitcast(I32),
+                )
+
+        def load_words(words):
+            passes = words.shape[0]
+            nc.sync.dma_start(out=w_raw[:, 0:passes, :].bitcast(I32), in_=words.rearrange("o p c -> p o c").bitcast(I32))
+
+        def deal_words(name, passes):
+            dealt = keep.tile([P, passes, PACK, 2 * P], U8, name=name, align_bytes=64)
+            for o in range(passes):
+                nc.vector.tensor_copy(
+                    out=dealt[:, o].rearrange("p t (m b) -> p t m b", b=2),
+                    in_=w_raw[:, o, :].rearrange("p (m t b) -> p t m b", t=PACK, b=2),
+                )
+            return dealt
+
+        def deal_scales(name, passes):
+            dealt = keep.tile([P, passes, PACK, P], U8, name=name, align_bytes=64)
+            nc.vector.tensor_copy(
+                out=dealt[:], in_=ws_raw[:, 0:passes, :].rearrange("p o (m t) -> p o t m", t=PACK)
+            )
+            return dealt
+
+        nc.vector.memset(xs_tab[:].bitcast(I32), 0)
+        nc.gpsimd.memset(ws_raw[:].rearrange("p o c -> p (o c)").bitcast(I32), 0)
+
+        nc.sync.dma_start(offs_sb[:], offs)
+        load_words(w2_words)
+        nc.sync.dma_start(cle_sb[:], cle)
+        for o in range(PASSES):
+            nc.sync.dma_start(out=x_tab[o][:], in_=x_words[o].rearrange("p c r -> p (c r)").bitcast(I32))
+        for q in range(QUADS):
+            nc.scalar.dma_start(
+                out=xs_tab[32 * q : 32 * q + 8, :].bitcast(I32), in_=x_scales[:, 4 * q : 4 * q + 4, :].bitcast(I32)
+            )
+        load_scale_rows((nc.scalar, nc.scalar, nc.scalar, nc.gpsimd), ws_raw, w2_scales)
+        nc.gpsimd.dma_start(out=unit_sb[:], in_=unit.rearrange("(p t) one -> p (t one)", t=PACK))
+
+        xg = [keep.tile([P, S], U32, name=f"xg{o}", align_bytes=64) for o in range(PASSES)]
+        xgs = [keep.tile([P, S], U8, name=f"xgs{o}", align_bytes=64) for o in range(PASSES)]
+
+        w2d = deal_words("w2d", PASSES)
+        load_words(w1_words)
+        nc.gpsimd.memset(xgs[1][:].bitcast(I32), 0)
+        nc.vector.tensor_copy(out=xgs[0][:], in_=xs_tab[:].indirect(offs_sb[:]))
+        for q in range(QUADS):
+            nc.scalar.dma_start(
+                out=xgs[1][32 * q : 32 * q + 4, :].bitcast(I32), in_=xgs[0][32 * q + 4 : 32 * q + 8, :].bitcast(I32)
+            )
+        nc.vector.tensor_copy(out=xg[0][:], in_=x_tab[0][:].bitcast(U32).indirect(offs_sb[:]))
+        w2s = deal_scales("w2s", PASSES)
+        nc.vector.tensor_copy(out=xg[1][:], in_=x_tab[1][:].bitcast(U32).indirect(offs_sb[:]))
+
+        load_scale_rows([nc.sync] * QUADS, ws_raw, w1_scales)
+        w1d = deal_words("w1d", PASSES)
+        w1s = deal_scales("w1s", PASSES)
+        load_words(w3_words)
+        load_scale_rows([nc.sync] * QUADS, ws_raw, w3_scales)
+
+        half_sign = keep.tile([P, PACK], F32, name="half_sign")
+        sign_bf = keep.tile([P, PACK], BF16, name="sign_bf")
+        unit_abs = keep.tile([P, PACK], F32, name="unit_abs")
+        nc.vector.tensor_scalar(half_sign[:], unit_sb[:], 0.0, 0.5, op0=ALU.is_ge, op1=ALU.subtract)
+        nc.vector.tensor_scalar(sign_bf[:], half_sign[:], 2.0, None, op0=ALU.mult)
+        nc.vector.scalar_tensor_tensor(unit_abs[:], half_sign[:], 2.0, unit_sb[:], op0=ALU.mult, op1=ALU.mult)
+
+        def first_product(name, words, scales):
+            banks = [psum.tile([P, S], F32, name=f"{name}{t}") for t in range(PACK)]
+            for o in range(PASSES):
+                for t in range(PACK):
+                    nc.tensor.matmul_mx(
+                        out=banks[t][:],
+                        lhsT=words[:, o, t, :].bitcast(FP4X4),
+                        lhsT_scale=scales[:, o, t, :],
+                        rhs=xg[o][:].bitcast(FP8X4),
+                        rhs_scale=xgs[o][:],
+                        start=(o == 0),
+                        stop=(o == PASSES - 1),
+                    )
+            return banks
+
+        z_ps = first_product("bank_z", w2d, w2s)
+        y_ps = first_product("bank_y", w1d, w1s)
+
+        prod = keep.tile([P, PACK, S], F32, name="prod")
+        for t in range(PACK):
+            z_sb = keep.tile([P, S], F32, name=f"z_sb{t}")
+            zc = keep.tile([P, S], F32, name=f"zc{t}")
+            nc.scalar.copy(out=z_sb[:], in_=z_ps[t][:])
+            for h in range(2):
+                cols = slice(h * HALF, (h + 1) * HALF)
+                picked = z_sb[:].indirect(cle_sb[:, h * HALF // 16 : (h + 1) * HALF // 16])
+                if (t, h) in VECTOR_GATHERS:
+                    nc.vector.tensor_copy(out=zc[:, cols], in_=picked)
+                else:
+                    nc.scalar.activation(zc[:, cols], picked, COPY)
+            nc.vector.scalar_tensor_tensor(
+                prod[:, t, :], y_ps[t][:], unit_abs[:, t : t + 1], zc[:], op0=ALU.mult, op1=ALU.mult
+            )
+
+        w3d = deal_words("w3d", 1)
+        w3s = deal_scales("w3s", 1)
+
+        out_codes = keep.tile([P, S], U32, name="out_codes", align_bytes=64)
+        out_scales = keep.tile([P, S], U8, name="out_scales", align_bytes=64)
+        out_rows = out_0.rearrange("(p t) c -> p t c", t=PACK)
+        out_words = out_1[0].rearrange("p c r -> p (c r)").bitcast(I32)
+
+        bank = 0
+        c0 = 0
+        for ci, n in enumerate(CHUNKS):
+            cols = slice(c0, c0 + n)
+            callee = keep.tile([P, PACK, n], F32, name=f"callee{ci}")
+            for t in range(PACK):
+                nc.scalar.activation(
+                    callee[:, t, :], prod[:, t, :].indirect(cle_sb[:, c0 // 16 : (c0 + n) // 16]), COPY
+                )
+            larger = keep.tile([P, n * PACK], BF16, name=f"larger{ci}")
+            nc.vector.tensor_tensor(
+                larger[:].rearrange("p (c i t) -> p c t i", i=4, t=PACK),
+                prod[:, :, cols].rearrange("p t (c i) -> p c t i", i=4),
+                callee[:].rearrange("p t (c i) -> p c t i", i=4),
+                ALU.max,
+            )
+            hid = keep.tile([P, n * PACK], BF16, name=f"hid{ci}", align_bytes=64)
+            nc.vector.tensor_tensor(
+                hid[:].rearrange("p (j t) -> p j t", t=PACK),
+                larger[:].rearrange("p (j t) -> p j t", t=PACK),
+                sign_bf[:].unsqueeze(1).to_broadcast([P, n, PACK]),
+                ALU.mult,
+            )
+            hq = keep.tile([P, n], U32, name=f"hq{ci}", align_bytes=64)
+            hs = keep.tile([P, n], U8, name=f"hs{ci}", align_bytes=64)
+            nc.vector.quantize_mx(out=hq[:].bitcast(FP8X4), scales=hs[:], in_=hid[:])
+
+            res = keep.tile([P, PACK, n], F32, name=f"res{ci}")
+            per_bank = S // n
+            for t0 in range(0, PACK, per_bank):
+                acc = psum.tile([P, per_bank, n], F32, name=f"bank_z{bank}")
+                bank = bank + 1
+                for t in range(t0, t0 + per_bank):
+                    nc.tensor.matmul_mx(
+                        out=acc[:, t - t0, :],
+                        lhsT=w3d[:, 0, t, :].bitcast(FP4X4),
+                        lhsT_scale=w3s[:, 0, t, :],
+                        rhs=hq[:].bitcast(FP8X4),
+                        rhs_scale=hs[:],
+                        start=True,
+                        stop=True,
+                    )
+                nc.scalar.copy(out=res[:, t0 : t0 + per_bank, :], in_=acc[:])
+            nc.sync.dma_start(out=out_rows[:, :, cols], in_=res[:])
+
+            res_bf = keep.tile([P, n * PACK], BF16, name=f"res_bf{ci}", align_bytes=64)
+            nc.vector.tensor_copy(
+                out=res_bf[:].rearrange("p (c i t) -> p c t i", i=4, t=PACK),
+                in_=res[:].rearrange("p t (c i) -> p c t i", i=4),
+            )
+            nc.vector.quantize_mx(out=out_codes[:, cols].bitcast(FP8X4), scales=out_scales[:, cols], in_=res_bf[:])
+            nc.sync.dma_start(out=out_words[:, cols], in_=out_codes[:, cols].bitcast(I32))
+            c0 = c0 + n
+
+        for q in range(QUADS):
+            queue = nc.sync if q % 2 == 0 else nc.scalar
+            queue.dma_start(
+                out=out_2[0, 4 * q : 4 * q + 4, :].bitcast(I32), in_=out_scales[32 * q : 32 * q + 4, :].bitcast(I32)
+            )

@@ -21,8 +21,7 @@ PACK = 4
 PASSES = K // (P * PACK)
 QUADS = 4
 HALF = S // 2
-CHUNKS = (256, 128, 128)
-VECTOR_GATHERS = ((1, 0), (1, 1), (3, 1))
+CHUNKS = (128, 256, 128)
 
 
 def tile_picked_ycallgr_max_po_kernel(
@@ -38,119 +37,142 @@ def tile_picked_ycallgr_max_po_kernel(
         offs_sb = lists.tile([P, S // 16], U16, name="offs_sb")
         cle_sb = lists.tile([P, S // 16], U16, name="cle_sb")
         x_tab = [keep.tile([P, T], I32, name=f"x_tab{o}") for o in range(PASSES)]
-        xs_tab = keep.tile([P, T], U8, name="xs_tab")
-        w_raw = keep.tile([P, PASSES, 2 * H], U8, name="w_raw")
-        ws_raw = keep.tile([P, PASSES, H], U8, name="ws_raw")
+        xs_tab = keep.tile([P, PASSES, T], U8, name="xs_tab")
+        ws_raw = keep.tile([P, 2 * PASSES + 1, H], U8, name="ws_raw")
+        w2s_raw, w1s_raw, w3s_raw = ws_raw[:, 0:2, :], ws_raw[:, 2:4, :], ws_raw[:, 4:5, :]
         unit_sb = keep.tile([P, PACK], F32, name="unit_sb")
 
-        def load_scale_rows(queues, tile, scales):
-            passes = scales.shape[0]
-            for q in range(QUADS):
-                queues[q].dma_start(
-                    out=tile[32 * q : 32 * q + 4, 0:passes, :].bitcast(I32),
+        def load_scale_rows(queue, tile, scales, quads=range(QUADS)):
+            for q in quads:
+                queue.dma_start(
+                    out=tile[32 * q : 32 * q + 4, :, :].bitcast(I32),
                     in_=scales[:, 4 * q : 4 * q + 4, :].rearrange("o r c -> r o c").bitcast(I32),
                 )
 
-        def load_words(words):
-            passes = words.shape[0]
-            nc.sync.dma_start(out=w_raw[:, 0:passes, :].bitcast(I32), in_=words.rearrange("o p c -> p o c").bitcast(I32))
+        def load_words(name, words):
+            raw = keep.tile([P, words.shape[0], 2 * H], U8, name=name)
+            nc.sync.dma_start(out=raw[:].bitcast(I32), in_=words.rearrange("o p c -> p o c").bitcast(I32))
+            return raw
 
-        def deal_words(name, passes):
+        def deal_words(name, w_raw, copy):
+            passes = w_raw.shape[1]
             dealt = keep.tile([P, passes, PACK, 2 * P], U8, name=name, align_bytes=64)
             for o in range(passes):
-                nc.vector.tensor_copy(
-                    out=dealt[:, o].rearrange("p t (m b) -> p t m b", b=2),
-                    in_=w_raw[:, o, :].rearrange("p (m t b) -> p t m b", t=PACK, b=2),
+                copy(
+                    out=dealt[:, o].bitcast(U16),
+                    in_=w_raw[:, o, :].bitcast(U16).rearrange("p (m t) -> p t m", t=PACK),
                 )
             return dealt
 
-        def deal_scales(name, passes):
+        def deal_scales(name, raw):
+            passes = raw.shape[1]
             dealt = keep.tile([P, passes, PACK, P], U8, name=name, align_bytes=64)
             nc.vector.tensor_copy(
-                out=dealt[:], in_=ws_raw[:, 0:passes, :].rearrange("p o (m t) -> p o t m", t=PACK)
+                out=dealt[:], in_=raw.rearrange("p o (m t) -> p o t m", t=PACK)
             )
             return dealt
 
-        nc.vector.memset(xs_tab[:].bitcast(I32), 0)
+        nc.gpsimd.memset(xs_tab[:, 0, :].bitcast(I32), 0)
+        nc.vector.memset(xs_tab[:, 1, :].bitcast(I32), 0)
         nc.gpsimd.memset(ws_raw[:].rearrange("p o c -> p (o c)").bitcast(I32), 0)
 
         nc.sync.dma_start(offs_sb[:], offs)
-        load_words(w2_words)
+        w2_raw = load_words("w2_raw", w2_words)
+        w1_raw = load_words("w1_raw", w1_words)
+        load_scale_rows(nc.sync, xs_tab, x_scales)
+        nc.sync.dma_start(out=x_tab[0][:], in_=x_words[0].rearrange("p c r -> p (c r)").bitcast(I32))
+        load_scale_rows(nc.sync, w2s_raw, w2_scales)
+        load_scale_rows(nc.sync, w1s_raw, w1_scales, (0, 1))
+        nc.sync.dma_start(out=x_tab[1][:], in_=x_words[1].rearrange("p c r -> p (c r)").bitcast(I32))
+        w3_raw = load_words("w3_raw", w3_words)
         nc.sync.dma_start(cle_sb[:], cle)
-        for o in range(PASSES):
-            nc.sync.dma_start(out=x_tab[o][:], in_=x_words[o].rearrange("p c r -> p (c r)").bitcast(I32))
-        for q in range(QUADS):
-            nc.scalar.dma_start(
-                out=xs_tab[32 * q : 32 * q + 8, :].bitcast(I32), in_=x_scales[:, 4 * q : 4 * q + 4, :].bitcast(I32)
-            )
-        load_scale_rows((nc.scalar, nc.scalar, nc.scalar, nc.gpsimd), ws_raw, w2_scales)
+        load_scale_rows(nc.gpsimd, w1s_raw, w1_scales, (2, 3))
         nc.gpsimd.dma_start(out=unit_sb[:], in_=unit.rearrange("(p t) one -> p (t one)", t=PACK))
+        load_scale_rows(nc.sync, w3s_raw, w3_scales)
 
         xg = [keep.tile([P, S], U32, name=f"xg{o}", align_bytes=64) for o in range(PASSES)]
         xgs = [keep.tile([P, S], U8, name=f"xgs{o}", align_bytes=64) for o in range(PASSES)]
 
-        w2d = deal_words("w2d", PASSES)
-        load_words(w1_words)
-        nc.gpsimd.memset(xgs[1][:].bitcast(I32), 0)
-        nc.vector.tensor_copy(out=xgs[0][:], in_=xs_tab[:].indirect(offs_sb[:]))
-        for q in range(QUADS):
-            nc.scalar.dma_start(
-                out=xgs[1][32 * q : 32 * q + 4, :].bitcast(I32), in_=xgs[0][32 * q + 4 : 32 * q + 8, :].bitcast(I32)
-            )
+        w2d = deal_words("w2d", w2_raw, nc.scalar.copy)
+        for o in range(PASSES):
+            nc.vector.tensor_copy(out=xgs[o][:], in_=xs_tab[:, o, :].indirect(offs_sb[:]))
         nc.vector.tensor_copy(out=xg[0][:], in_=x_tab[0][:].bitcast(U32).indirect(offs_sb[:]))
-        w2s = deal_scales("w2s", PASSES)
+        w2s = deal_scales("w2s", w2s_raw)
+        w1s = deal_scales("w1s", w1s_raw)
         nc.vector.tensor_copy(out=xg[1][:], in_=x_tab[1][:].bitcast(U32).indirect(offs_sb[:]))
 
-        load_scale_rows([nc.sync] * QUADS, ws_raw, w1_scales)
-        w1d = deal_words("w1d", PASSES)
-        w1s = deal_scales("w1s", PASSES)
-        load_words(w3_words)
-        load_scale_rows([nc.sync] * QUADS, ws_raw, w3_scales)
+        w1d = deal_words("w1d", w1_raw, nc.scalar.copy)
+        w3d = deal_words("w3d", w3_raw, nc.scalar.copy)
 
         half_sign = keep.tile([P, PACK], F32, name="half_sign")
+        sign = keep.tile([P, PACK], F32, name="sign")
         sign_bf = keep.tile([P, PACK], BF16, name="sign_bf")
         unit_abs = keep.tile([P, PACK], F32, name="unit_abs")
-        nc.vector.tensor_scalar(half_sign[:], unit_sb[:], 0.0, 0.5, op0=ALU.is_ge, op1=ALU.subtract)
-        nc.vector.tensor_scalar(sign_bf[:], half_sign[:], 2.0, None, op0=ALU.mult)
-        nc.vector.scalar_tensor_tensor(unit_abs[:], half_sign[:], 2.0, unit_sb[:], op0=ALU.mult, op1=ALU.mult)
+        nc.gpsimd.tensor_scalar(half_sign[:], unit_sb[:], 0.0, 0.5, op0=ALU.is_ge, op1=ALU.subtract)
+        nc.gpsimd.tensor_scalar(sign[:], half_sign[:], 2.0, 0.0, op0=ALU.mult, op1=ALU.add)
+        nc.gpsimd.tensor_tensor(unit_abs[:], sign[:], unit_sb[:], ALU.mult)
+        nc.gpsimd.tensor_copy(out=sign_bf[:], in_=sign[:])
 
-        def first_product(name, words, scales):
-            banks = [psum.tile([P, S], F32, name=f"{name}{t}") for t in range(PACK)]
-            for o in range(PASSES):
-                for t in range(PACK):
-                    nc.tensor.matmul_mx(
-                        out=banks[t][:],
-                        lhsT=words[:, o, t, :].bitcast(FP4X4),
-                        lhsT_scale=scales[:, o, t, :],
-                        rhs=xg[o][:].bitcast(FP8X4),
-                        rhs_scale=xgs[o][:],
-                        start=(o == 0),
-                        stop=(o == PASSES - 1),
-                    )
-            return banks
+        z_ps = [psum.tile([P, S], F32, name=f"bank_z{t}") for t in range(PACK)]
+        y_ps = [psum.tile([P, S], F32, name=f"bank_y{t}") for t in range(PACK)]
 
-        z_ps = first_product("bank_z", w2d, w2s)
-        y_ps = first_product("bank_y", w1d, w1s)
-
-        prod = keep.tile([P, PACK, S], F32, name="prod")
-        for t in range(PACK):
-            z_sb = keep.tile([P, S], F32, name=f"z_sb{t}")
-            zc = keep.tile([P, S], F32, name=f"zc{t}")
-            nc.scalar.copy(out=z_sb[:], in_=z_ps[t][:])
-            for h in range(2):
-                cols = slice(h * HALF, (h + 1) * HALF)
-                picked = z_sb[:].indirect(cle_sb[:, h * HALF // 16 : (h + 1) * HALF // 16])
-                if (t, h) in VECTOR_GATHERS:
-                    nc.vector.tensor_copy(out=zc[:, cols], in_=picked)
-                else:
-                    nc.scalar.activation(zc[:, cols], picked, COPY)
-            nc.vector.scalar_tensor_tensor(
-                prod[:, t, :], y_ps[t][:], unit_abs[:, t : t + 1], zc[:], op0=ALU.mult, op1=ALU.mult
+        def one_pass(bank, words, scales, t, o, first=0):
+            nc.tensor.matmul_mx(
+                out=bank[:],
+                lhsT=words[:, o, t, :].bitcast(FP4X4),
+                lhsT_scale=scales[:, o, t, :],
+                rhs=xg[o][:].bitcast(FP8X4),
+                rhs_scale=xgs[o][:],
+                start=(o == first),
+                stop=(o != first),
             )
 
-        w3d = deal_words("w3d", 1)
-        w3s = deal_scales("w3s", 1)
+        for t in range(PACK):
+            one_pass(z_ps[t], w2d, w2s, t, 0)
+        for t in range(PACK + 1):
+            if t < PACK:
+                one_pass(z_ps[t], w2d, w2s, t, 1)
+            if t > 0:
+                for o in reversed(range(PASSES)):
+                    one_pass(y_ps[t - 1], w1d, w1s, t - 1, o, first=1)
 
+        prod = keep.tile([P, PACK, S], F32, name="prod")
+        z_sb = [keep.tile([P, S], F32, name=f"z_sb{t}", align_bytes=64) for t in range(PACK)]
+        zc = [keep.tile([P, S], F32, name=f"zc{t}", align_bytes=64) for t in range(PACK)]
+
+        def gather(on_vector, out, window, c0, n):
+            picked = window.indirect(cle_sb[:, c0 // 16 : (c0 + n) // 16])
+            if on_vector:
+                nc.vector.tensor_copy(out=out, in_=picked)
+            else:
+                nc.scalar.activation(out, picked, COPY)
+
+        def z_out(t):
+            nc.scalar.copy(out=z_sb[t][:], in_=z_ps[t][:])
+
+        def z_gather(t):
+            for c0 in (0, HALF):
+                gather(t % 2 == 0, zc[t][:, c0 : c0 + HALF], z_sb[t][:], c0, HALF)
+
+        def multiply(t):
+            nc.vector.scalar_tensor_tensor(
+                prod[:, t, :], y_ps[t][:], unit_abs[:, t : t + 1], zc[t][:], op0=ALU.mult, op1=ALU.mult
+            )
+
+        z_out(0)
+        z_out(1)
+        z_out(2)
+        z_gather(0)
+        multiply(0)
+        z_gather(1)
+        z_out(3)
+        z_gather(2)
+        multiply(1)
+        multiply(2)
+        z_gather(3)
+        multiply(3)
+
+        w3s = deal_scales("zc1", w3s_raw)
         out_codes = keep.tile([P, S], U32, name="out_codes", align_bytes=64)
         out_scales = keep.tile([P, S], U8, name="out_scales", align_bytes=64)
         out_rows = out_0.rearrange("(p t) c -> p t c", t=PACK)
@@ -160,22 +182,19 @@ def tile_picked_ycallgr_max_po_kernel(
         c0 = 0
         for ci, n in enumerate(CHUNKS):
             cols = slice(c0, c0 + n)
-            callee = keep.tile([P, PACK, n], F32, name=f"callee{ci}")
+            callee = keep.tile([P, PACK, n], F32, name=("z_sb3", "zc3")[ci % 2], align_bytes=64)
             for t in range(PACK):
-                nc.scalar.activation(
-                    callee[:, t, :], prod[:, t, :].indirect(cle_sb[:, c0 // 16 : (c0 + n) // 16]), COPY
-                )
-            larger = keep.tile([P, n * PACK], BF16, name=f"larger{ci}")
+                gather(t == PACK - 1 and ci < 2, callee[:, t, :], prod[:, t, :], c0, n)
+            hid = keep.tile([P, n * PACK], BF16, name="hid", align_bytes=64)
             nc.vector.tensor_tensor(
-                larger[:].rearrange("p (c i t) -> p c t i", i=4, t=PACK),
+                hid[:].rearrange("p (c i t) -> p c t i", i=4, t=PACK),
                 prod[:, :, cols].rearrange("p t (c i) -> p c t i", i=4),
                 callee[:].rearrange("p t (c i) -> p c t i", i=4),
                 ALU.max,
             )
-            hid = keep.tile([P, n * PACK], BF16, name=f"hid{ci}", align_bytes=64)
             nc.vector.tensor_tensor(
                 hid[:].rearrange("p (j t) -> p j t", t=PACK),
-                larger[:].rearrange("p (j t) -> p j t", t=PACK),
+                hid[:].rearrange("p (j t) -> p j t", t=PACK),
                 sign_bf[:].unsqueeze(1).to_broadcast([P, n, PACK]),
                 ALU.mult,
             )

@@ -42,11 +42,11 @@ def tile_picked_ycallgr_max_po_kernel(
         w2s_raw, w1s_raw, w3s_raw = ws_raw[:, 0:2, :], ws_raw[:, 2:4, :], ws_raw[:, 4:5, :]
         unit_sb = keep.tile([P, PACK], F32, name="unit_sb")
 
-        def load_scale_rows(queue, tile, scales, quads=range(QUADS)):
-            for q in quads:
+        def load_scale_rows(queue, tile, scales, rows=range(4)):
+            for r in rows:
                 queue.dma_start(
-                    out=tile[32 * q : 32 * q + 4, :, :].bitcast(I32),
-                    in_=scales[:, 4 * q : 4 * q + 4, :].rearrange("o r c -> r o c").bitcast(I32),
+                    out=tile[r:P:32, :, :].bitcast(I32),
+                    in_=scales.rearrange("o (q r) c -> r q o c", r=4)[r].bitcast(I32),
                 )
 
         def load_words(name, words):
@@ -187,9 +187,9 @@ def tile_picked_ycallgr_max_po_kernel(
                 gather(t == PACK - 1 and ci < 2, callee[:, t, :], prod[:, t, :], c0, n)
             hid = keep.tile([P, n * PACK], BF16, name="hid", align_bytes=64)
             nc.vector.tensor_tensor(
-                hid[:].rearrange("p (c i t) -> p c t i", i=4, t=PACK),
-                prod[:, :, cols].rearrange("p t (c i) -> p c t i", i=4),
-                callee[:].rearrange("p t (c i) -> p c t i", i=4),
+                hid[:].rearrange("p (c i t) -> p c t i", i=2, t=PACK),
+                prod[:, :, cols].rearrange("p t (c i) -> p c t i", i=2),
+                callee[:].rearrange("p t (c i) -> p c t i", i=2),
                 ALU.max,
             )
             nc.vector.tensor_tensor(
@@ -222,15 +222,15 @@ def tile_picked_ycallgr_max_po_kernel(
 
             res_bf = keep.tile([P, n * PACK], BF16, name=f"res_bf{ci}", align_bytes=64)
             nc.vector.tensor_copy(
-                out=res_bf[:].rearrange("p (c i t) -> p c t i", i=4, t=PACK),
-                in_=res[:].rearrange("p t (c i) -> p c t i", i=4),
+                out=res_bf[:].rearrange("p (c i t) -> p c t i", i=2, t=PACK),
+                in_=res[:].rearrange("p t (c i) -> p c t i", i=2),
             )
             nc.vector.quantize_mx(out=out_codes[:, cols].bitcast(FP8X4), scales=out_scales[:, cols], in_=res_bf[:])
             nc.sync.dma_start(out=out_words[:, cols], in_=out_codes[:, cols].bitcast(I32))
             c0 = c0 + n
 
-        for q in range(QUADS):
-            queue = nc.sync if q % 2 == 0 else nc.scalar
+        for r in range(4):
+            queue = nc.sync if r % 2 == 0 else nc.scalar
             queue.dma_start(
-                out=out_2[0, 4 * q : 4 * q + 4, :].bitcast(I32), in_=out_scales[32 * q : 32 * q + 4, :].bitcast(I32)
+                out=out_2[0].rearrange("(q r) c -> r q c", r=4)[r].bitcast(I32), in_=out_scales[r:P:32, :].bitcast(I32)
             )

@@ -21,7 +21,7 @@ PACK = 4
 PASSES = K // (P * PACK)
 QUADS = 4
 HALF = S // 2
-CHUNKS = (128, 256, 128)
+CHUNK = 128
 
 
 def tile_picked_ycallgr_max_po_kernel(
@@ -32,6 +32,7 @@ def tile_picked_ycallgr_max_po_kernel(
     with ExitStack() as ctx:
         lists = ctx.enter_context(tc.tile_pool(name="lists", bufs=1))
         keep = ctx.enter_context(tc.tile_pool(name="keep", bufs=1))
+        ring = ctx.enter_context(tc.tile_pool(name="ring", bufs=2))
         psum = ctx.enter_context(tc.psum_pool(name="psum", bufs=1))
 
         offs_sb = lists.tile([P, S // 16], U16, name="offs_sb")
@@ -64,6 +65,16 @@ def tile_picked_ycallgr_max_po_kernel(
                 )
             return dealt
 
+        def deal_words_as_bytes(name, w_raw):
+            passes = w_raw.shape[1]
+            dealt = keep.tile([P, passes, PACK, 2 * P], U8, name=name, align_bytes=64)
+            for o in reversed(range(passes)):
+                nc.vector.tensor_copy(
+                    out=dealt[:, o].rearrange("p t (m b) -> p t m b", b=2),
+                    in_=w_raw[:, o, :].rearrange("p (m t b) -> p t m b", t=PACK, b=2),
+                )
+            return dealt
+
         def deal_scales(name, raw):
             passes = raw.shape[1]
             dealt = keep.tile([P, passes, PACK, P], U8, name=name, align_bytes=64)
@@ -74,17 +85,17 @@ def tile_picked_ycallgr_max_po_kernel(
 
         nc.gpsimd.memset(xs_tab[:, 0, :].bitcast(I32), 0)
         nc.vector.memset(xs_tab[:, 1, :].bitcast(I32), 0)
-        nc.gpsimd.memset(ws_raw[:].rearrange("p o c -> p (o c)").bitcast(I32), 0)
+        nc.vector.memset(ws_raw[:].rearrange("p o c -> p (o c)").bitcast(I32), 0)
 
         nc.sync.dma_start(offs_sb[:], offs)
         w2_raw = load_words("w2_raw", w2_words)
-        w1_raw = load_words("w1_raw", w1_words)
+        w3_raw = load_words("w3_raw", w3_words)
         load_scale_rows(nc.sync, xs_tab, x_scales)
         nc.sync.dma_start(out=x_tab[0][:], in_=x_words[0].rearrange("p c r -> p (c r)").bitcast(I32))
         load_scale_rows(nc.sync, w2s_raw, w2_scales)
         load_scale_rows(nc.sync, w1s_raw, w1_scales, (0, 1))
         nc.sync.dma_start(out=x_tab[1][:], in_=x_words[1].rearrange("p c r -> p (c r)").bitcast(I32))
-        w3_raw = load_words("w3_raw", w3_words)
+        w1_raw = load_words("w1_raw", w1_words)
         nc.sync.dma_start(cle_sb[:], cle)
         load_scale_rows(nc.gpsimd, w1s_raw, w1_scales, (2, 3))
         nc.gpsimd.dma_start(out=unit_sb[:], in_=unit.rearrange("(p t) one -> p (t one)", t=PACK))
@@ -101,7 +112,7 @@ def tile_picked_ycallgr_max_po_kernel(
         w1s = deal_scales("w1s", w1s_raw)
         nc.vector.tensor_copy(out=xg[1][:], in_=x_tab[1][:].bitcast(U32).indirect(offs_sb[:]))
 
-        w1d = deal_words("w1d", w1_raw, nc.scalar.copy)
+        w1d = deal_words_as_bytes("w1d", w1_raw)
         w3d = deal_words("w3d", w3_raw, nc.scalar.copy)
 
         half_sign = keep.tile([P, PACK], F32, name="half_sign")
@@ -163,14 +174,12 @@ def tile_picked_ycallgr_max_po_kernel(
         z_out(1)
         z_out(2)
         z_gather(0)
-        multiply(0)
         z_gather(1)
         z_out(3)
         z_gather(2)
-        multiply(1)
-        multiply(2)
         z_gather(3)
-        multiply(3)
+        for t in range(PACK):
+            multiply(t)
 
         w3s = deal_scales("zc1", w3s_raw)
         out_codes = keep.tile([P, S], U32, name="out_codes", align_bytes=64)
@@ -178,38 +187,35 @@ def tile_picked_ycallgr_max_po_kernel(
         out_rows = out_0.rearrange("(p t) c -> p t c", t=PACK)
         out_words = out_1[0].rearrange("p c r -> p (c r)").bitcast(I32)
 
-        bank = 0
-        c0 = 0
-        for ci, n in enumerate(CHUNKS):
-            cols = slice(c0, c0 + n)
-            callee = keep.tile([P, PACK, n], F32, name=("z_sb3", "zc3")[ci % 2], align_bytes=64)
+        def second_product(half):
+            callee = keep.tile([P, PACK, HALF], F32, name=("z_sb3", "zc3")[half], align_bytes=64)
             for t in range(PACK):
-                gather(t == PACK - 1 and ci < 2, callee[:, t, :], prod[:, t, :], c0, n)
-            hid = keep.tile([P, n * PACK], BF16, name="hid", align_bytes=64)
-            nc.vector.tensor_tensor(
-                hid[:].rearrange("p (c i t) -> p c t i", i=2, t=PACK),
-                prod[:, :, cols].rearrange("p t (c i) -> p c t i", i=2),
-                callee[:].rearrange("p t (c i) -> p c t i", i=2),
-                ALU.max,
-            )
-            nc.vector.tensor_tensor(
-                hid[:].rearrange("p (j t) -> p j t", t=PACK),
-                hid[:].rearrange("p (j t) -> p j t", t=PACK),
-                sign_bf[:].unsqueeze(1).to_broadcast([P, n, PACK]),
-                ALU.mult,
-            )
-            hq = keep.tile([P, n], U32, name=f"hq{ci}", align_bytes=64)
-            hs = keep.tile([P, n], U8, name=f"hs{ci}", align_bytes=64)
-            nc.vector.quantize_mx(out=hq[:].bitcast(FP8X4), scales=hs[:], in_=hid[:])
-
-            res = keep.tile([P, PACK, n], F32, name=f"res{ci}")
-            per_bank = S // n
-            for t0 in range(0, PACK, per_bank):
-                acc = psum.tile([P, per_bank, n], F32, name=f"bank_z{bank}")
-                bank = bank + 1
-                for t in range(t0, t0 + per_bank):
+                gather(t == PACK - 1 and half == 0, callee[:, t, :], prod[:, t, :], half * HALF, HALF)
+            chunks = range(2 * half, 2 * half + 2)
+            hid = {ci: ring.tile([P, CHUNK * PACK], BF16, name="hid", align_bytes=64) for ci in chunks}
+            for ci in chunks:
+                nc.vector.tensor_tensor(
+                    hid[ci][:].rearrange("p (c i t) -> p c t i", i=2, t=PACK),
+                    prod[:, :, ci * CHUNK : (ci + 1) * CHUNK].rearrange("p t (c i) -> p c t i", i=2),
+                    callee[:, :, ci % 2 * CHUNK : (ci % 2 + 1) * CHUNK].rearrange("p t (c i) -> p c t i", i=2),
+                    ALU.max,
+                )
+            for ci in chunks:
+                nc.vector.tensor_tensor(
+                    hid[ci][:].rearrange("p (j t) -> p j t", t=PACK),
+                    hid[ci][:].rearrange("p (j t) -> p j t", t=PACK),
+                    sign_bf[:].unsqueeze(1).to_broadcast([P, CHUNK, PACK]),
+                    ALU.mult,
+                )
+            accs = []
+            for ci in chunks:
+                hq = keep.tile([P, CHUNK], U32, name=f"hq{ci}", align_bytes=64)
+                hs = keep.tile([P, CHUNK], U8, name=f"hs{ci}", align_bytes=64)
+                nc.vector.quantize_mx(out=hq[:].bitcast(FP8X4), scales=hs[:], in_=hid[ci][:])
+                acc = psum.tile([P, PACK, CHUNK], F32, name=f"bank_z{ci}")
+                for t in range(PACK):
                     nc.tensor.matmul_mx(
-                        out=acc[:, t - t0, :],
+                        out=acc[:, t, :],
                         lhsT=w3d[:, 0, t, :].bitcast(FP4X4),
                         lhsT_scale=w3s[:, 0, t, :],
                         rhs=hq[:].bitcast(FP8X4),
@@ -217,17 +223,25 @@ def tile_picked_ycallgr_max_po_kernel(
                         start=True,
                         stop=True,
                     )
-                nc.scalar.copy(out=res[:, t0 : t0 + per_bank, :], in_=acc[:])
-            nc.sync.dma_start(out=out_rows[:, :, cols], in_=res[:])
+                accs.append(acc)
+            return accs
 
-            res_bf = keep.tile([P, n * PACK], BF16, name=f"res_bf{ci}", align_bytes=64)
+        def hand_out(ci, acc):
+            cols = slice(ci * CHUNK, (ci + 1) * CHUNK)
+            res = keep.tile([P, PACK, CHUNK], F32, name=f"res{ci}")
+            nc.scalar.copy(out=res[:], in_=acc[:])
+            nc.sync.dma_start(out=out_rows[:, :, cols], in_=res[:])
+            res_bf = keep.tile([P, CHUNK * PACK], BF16, name=f"res_bf{ci}", align_bytes=64)
             nc.vector.tensor_copy(
                 out=res_bf[:].rearrange("p (c i t) -> p c t i", i=2, t=PACK),
                 in_=res[:].rearrange("p t (c i) -> p c t i", i=2),
             )
             nc.vector.quantize_mx(out=out_codes[:, cols].bitcast(FP8X4), scales=out_scales[:, cols], in_=res_bf[:])
             nc.sync.dma_start(out=out_words[:, cols], in_=out_codes[:, cols].bitcast(I32))
-            c0 = c0 + n
+
+        accs = second_product(0) + second_product(1)
+        for ci in range(4):
+            hand_out(ci, accs[ci])
 
         for r in range(4):
             queue = nc.sync if r % 2 == 0 else nc.scalar

@@ -14,14 +14,17 @@ U8 = mybir.dt.uint8
 FP8X4 = mybir.dt.float8_e4m3fn_x4
 FP4X4 = mybir.dt.float4_e2m1fn_x4
 ALU = mybir.AluOpType
-COPY = mybir.ActivationFunctionType.Copy
+ACT = mybir.ActivationFunctionType
 
 P = 128
 PACK = 4
 PASSES = K // (P * PACK)
-QUADS = 4
+SCALE_ROWS = 4
+LIST_ROWS = 16
 HALF = S // 2
 CHUNK = 128
+CHUNKS = S // CHUNK
+PAIR = 2
 
 
 def tile_picked_ycallgr_max_po_kernel(
@@ -35,19 +38,21 @@ def tile_picked_ycallgr_max_po_kernel(
         ring = ctx.enter_context(tc.tile_pool(name="ring", bufs=2))
         psum = ctx.enter_context(tc.psum_pool(name="psum", bufs=1))
 
-        offs_sb = lists.tile([P, S // 16], U16, name="offs_sb")
-        cle_sb = lists.tile([P, S // 16], U16, name="cle_sb")
+        offs_sb = lists.tile([P, S // LIST_ROWS], U16, name="offs_sb")
+        cle_sb = lists.tile([P, S // LIST_ROWS], U16, name="cle_sb")
         x_tab = [keep.tile([P, T], I32, name=f"x_tab{o}") for o in range(PASSES)]
         xs_tab = keep.tile([P, PASSES, T], U8, name="xs_tab")
         ws_raw = keep.tile([P, 2 * PASSES + 1, H], U8, name="ws_raw")
-        w2s_raw, w1s_raw, w3s_raw = ws_raw[:, 0:2, :], ws_raw[:, 2:4, :], ws_raw[:, 4:5, :]
+        w2s_raw = ws_raw[:, 0:PASSES, :]
+        w1s_raw = ws_raw[:, PASSES : 2 * PASSES, :]
+        w3s_raw = ws_raw[:, 2 * PASSES : 2 * PASSES + 1, :]
         unit_sb = keep.tile([P, PACK], F32, name="unit_sb")
 
-        def load_scale_rows(queue, tile, scales, rows=range(4)):
+        def load_scale_rows(queue, tile, scales, rows=range(SCALE_ROWS)):
             for r in rows:
                 queue.dma_start(
                     out=tile[r:P:32, :, :].bitcast(I32),
-                    in_=scales.rearrange("o (q r) c -> r q o c", r=4)[r].bitcast(I32),
+                    in_=scales.rearrange("o (q r) c -> r q o c", r=SCALE_ROWS)[r].bitcast(I32),
                 )
 
         def load_words(name, words):
@@ -55,17 +60,17 @@ def tile_picked_ycallgr_max_po_kernel(
             nc.sync.dma_start(out=raw[:].bitcast(I32), in_=words.rearrange("o p c -> p o c").bitcast(I32))
             return raw
 
-        def deal_words(name, w_raw, copy):
+        def deal_words_on_scalar(name, w_raw):
             passes = w_raw.shape[1]
             dealt = keep.tile([P, passes, PACK, 2 * P], U8, name=name, align_bytes=64)
             for o in range(passes):
-                copy(
+                nc.scalar.copy(
                     out=dealt[:, o].bitcast(U16),
                     in_=w_raw[:, o, :].bitcast(U16).rearrange("p (m t) -> p t m", t=PACK),
                 )
             return dealt
 
-        def deal_words_as_bytes(name, w_raw):
+        def deal_words_on_vector(name, w_raw):
             passes = w_raw.shape[1]
             dealt = keep.tile([P, passes, PACK, 2 * P], U8, name=name, align_bytes=64)
             for o in reversed(range(passes)):
@@ -78,9 +83,7 @@ def tile_picked_ycallgr_max_po_kernel(
         def deal_scales(name, raw):
             passes = raw.shape[1]
             dealt = keep.tile([P, passes, PACK, P], U8, name=name, align_bytes=64)
-            nc.vector.tensor_copy(
-                out=dealt[:], in_=raw.rearrange("p o (m t) -> p o t m", t=PACK)
-            )
+            nc.vector.tensor_copy(out=dealt[:], in_=raw.rearrange("p o (m t) -> p o t m", t=PACK))
             return dealt
 
         nc.gpsimd.memset(xs_tab[:, 0, :].bitcast(I32), 0)
@@ -104,7 +107,7 @@ def tile_picked_ycallgr_max_po_kernel(
         xg = [keep.tile([P, S], U32, name=f"xg{o}", align_bytes=64) for o in range(PASSES)]
         xgs = [keep.tile([P, S], U8, name=f"xgs{o}", align_bytes=64) for o in range(PASSES)]
 
-        w2d = deal_words("w2d", w2_raw, nc.scalar.copy)
+        w2d = deal_words_on_scalar("w2d", w2_raw)
         for o in range(PASSES):
             nc.vector.tensor_copy(out=xgs[o][:], in_=xs_tab[:, o, :].indirect(offs_sb[:]))
         nc.vector.tensor_copy(out=xg[0][:], in_=x_tab[0][:].bitcast(U32).indirect(offs_sb[:]))
@@ -112,22 +115,18 @@ def tile_picked_ycallgr_max_po_kernel(
         w1s = deal_scales("w1s", w1s_raw)
         nc.vector.tensor_copy(out=xg[1][:], in_=x_tab[1][:].bitcast(U32).indirect(offs_sb[:]))
 
-        w1d = deal_words_as_bytes("w1d", w1_raw)
-        w3d = deal_words("w3d", w3_raw, nc.scalar.copy)
+        w1d = deal_words_on_vector("w1d", w1_raw)
+        w3d = deal_words_on_scalar("w3d", w3_raw)
 
-        half_sign = keep.tile([P, PACK], F32, name="half_sign")
-        sign = keep.tile([P, PACK], F32, name="sign")
         sign_bf = keep.tile([P, PACK], BF16, name="sign_bf")
         unit_abs = keep.tile([P, PACK], F32, name="unit_abs")
-        nc.gpsimd.tensor_scalar(half_sign[:], unit_sb[:], 0.0, 0.5, op0=ALU.is_ge, op1=ALU.subtract)
-        nc.gpsimd.tensor_scalar(sign[:], half_sign[:], 2.0, 0.0, op0=ALU.mult, op1=ALU.add)
-        nc.gpsimd.tensor_tensor(unit_abs[:], sign[:], unit_sb[:], ALU.mult)
-        nc.gpsimd.tensor_copy(out=sign_bf[:], in_=sign[:])
+        nc.scalar.activation(unit_abs[:], unit_sb[:], ACT.Abs)
+        nc.scalar.activation(sign_bf[:], unit_sb[:], ACT.Sign)
 
         z_ps = [psum.tile([P, S], F32, name=f"bank_z{t}") for t in range(PACK)]
         y_ps = [psum.tile([P, S], F32, name=f"bank_y{t}") for t in range(PACK)]
 
-        def one_pass(bank, words, scales, t, o, first=0):
+        def one_pass(bank, words, scales, t, o, first):
             nc.tensor.matmul_mx(
                 out=bank[:],
                 lhsT=words[:, o, t, :].bitcast(FP4X4),
@@ -138,66 +137,53 @@ def tile_picked_ycallgr_max_po_kernel(
                 stop=(o != first),
             )
 
+        for o in range(PASSES):
+            for t in range(PACK):
+                one_pass(z_ps[t], w2d, w2s, t, o, first=0)
         for t in range(PACK):
-            one_pass(z_ps[t], w2d, w2s, t, 0)
-        for t in range(PACK + 1):
-            if t < PACK:
-                one_pass(z_ps[t], w2d, w2s, t, 1)
-            if t > 0:
-                for o in reversed(range(PASSES)):
-                    one_pass(y_ps[t - 1], w1d, w1s, t - 1, o, first=1)
+            for o in reversed(range(PASSES)):
+                one_pass(y_ps[t], w1d, w1s, t, o, first=PASSES - 1)
 
         prod = keep.tile([P, PACK, S], F32, name="prod")
         z_sb = [keep.tile([P, S], F32, name=f"z_sb{t}", align_bytes=64) for t in range(PACK)]
         zc = [keep.tile([P, S], F32, name=f"zc{t}", align_bytes=64) for t in range(PACK)]
 
-        def gather(on_vector, out, window, c0, n):
-            picked = window.indirect(cle_sb[:, c0 // 16 : (c0 + n) // 16])
+        def gather_half(on_vector, out, window, half):
+            picked = window.indirect(cle_sb[:, half * HALF // LIST_ROWS : (half + 1) * HALF // LIST_ROWS])
             if on_vector:
                 nc.vector.tensor_copy(out=out, in_=picked)
             else:
-                nc.scalar.activation(out, picked, COPY)
+                nc.scalar.activation(out, picked, ACT.Copy)
 
-        def z_out(t):
+        for t in range(PACK):
             nc.scalar.copy(out=z_sb[t][:], in_=z_ps[t][:])
-
-        def z_gather(t):
-            for c0 in (0, HALF):
-                gather(t % 2 == 0, zc[t][:, c0 : c0 + HALF], z_sb[t][:], c0, HALF)
-
-        def multiply(t):
+        for t in range(PACK):
+            for half in range(2):
+                gather_half(t % 2 == 0, zc[t][:, half * HALF : (half + 1) * HALF], z_sb[t][:], half)
+        for t in range(PACK):
             nc.vector.scalar_tensor_tensor(
                 prod[:, t, :], y_ps[t][:], unit_abs[:, t : t + 1], zc[t][:], op0=ALU.mult, op1=ALU.mult
             )
 
-        z_out(0)
-        z_out(1)
-        z_out(2)
-        z_gather(0)
-        z_gather(1)
-        z_out(3)
-        z_gather(2)
-        z_gather(3)
-        for t in range(PACK):
-            multiply(t)
-
-        w3s = deal_scales("zc1", w3s_raw)
+        w3s = deal_scales("zc2", w3s_raw)
         out_codes = keep.tile([P, S], U32, name="out_codes", align_bytes=64)
         out_scales = keep.tile([P, S], U8, name="out_scales", align_bytes=64)
         out_rows = out_0.rearrange("(p t) c -> p t c", t=PACK)
         out_words = out_1[0].rearrange("p c r -> p (c r)").bitcast(I32)
 
-        def second_product(half):
+        def last_product(half):
             callee = keep.tile([P, PACK, HALF], F32, name=("z_sb3", "zc3")[half], align_bytes=64)
             for t in range(PACK):
-                gather(t == PACK - 1 and half == 0, callee[:, t, :], prod[:, t, :], half * HALF, HALF)
-            chunks = range(2 * half, 2 * half + 2)
+                gather_half(t == 0 and half == 1, callee[:, t, :], prod[:, t, :], half)
+            per_half = HALF // CHUNK
+            chunks = range(per_half * half, per_half * (half + 1))
             hid = {ci: ring.tile([P, CHUNK * PACK], BF16, name="hid", align_bytes=64) for ci in chunks}
             for ci in chunks:
+                in_half = ci % per_half * CHUNK
                 nc.vector.tensor_tensor(
-                    hid[ci][:].rearrange("p (c i t) -> p c t i", i=2, t=PACK),
-                    prod[:, :, ci * CHUNK : (ci + 1) * CHUNK].rearrange("p t (c i) -> p c t i", i=2),
-                    callee[:, :, ci % 2 * CHUNK : (ci % 2 + 1) * CHUNK].rearrange("p t (c i) -> p c t i", i=2),
+                    hid[ci][:].rearrange("p (c i t) -> p c t i", i=PAIR, t=PACK),
+                    prod[:, :, ci * CHUNK : (ci + 1) * CHUNK].rearrange("p t (c i) -> p c t i", i=PAIR),
+                    callee[:, :, in_half : in_half + CHUNK].rearrange("p t (c i) -> p c t i", i=PAIR),
                     ALU.max,
                 )
             for ci in chunks:
@@ -212,10 +198,12 @@ def tile_picked_ycallgr_max_po_kernel(
                 hq = keep.tile([P, CHUNK], U32, name=f"hq{ci}", align_bytes=64)
                 hs = keep.tile([P, CHUNK], U8, name=f"hs{ci}", align_bytes=64)
                 nc.vector.quantize_mx(out=hq[:].bitcast(FP8X4), scales=hs[:], in_=hid[ci][:])
-                acc = psum.tile([P, PACK, CHUNK], F32, name=f"bank_z{ci}")
+                names = [f"bank_z{ci}"] if ci < CHUNKS - 1 else [f"bank_z{ci}", "bank_y0"]
+                per_bank = PACK // len(names)
+                acc = [psum.tile([P, per_bank, CHUNK], F32, name=name) for name in names]
                 for t in range(PACK):
                     nc.tensor.matmul_mx(
-                        out=acc[:, t, :],
+                        out=acc[t // per_bank][:, t % per_bank, :],
                         lhsT=w3d[:, 0, t, :].bitcast(FP4X4),
                         lhsT_scale=w3s[:, 0, t, :],
                         rhs=hq[:].bitcast(FP8X4),
@@ -229,22 +217,29 @@ def tile_picked_ycallgr_max_po_kernel(
         def hand_out(ci, acc):
             cols = slice(ci * CHUNK, (ci + 1) * CHUNK)
             res = keep.tile([P, PACK, CHUNK], F32, name=f"res{ci}")
-            nc.scalar.copy(out=res[:], in_=acc[:])
+            if len(acc) == 1:
+                nc.scalar.copy(out=res[:], in_=acc[0][:])
+            else:
+                nc.vector.tensor_copy(out=res[:, 0 : PACK // 2, :], in_=acc[0][:])
+                nc.scalar.copy(out=res[:, PACK // 2 : PACK, :], in_=acc[1][:])
             nc.sync.dma_start(out=out_rows[:, :, cols], in_=res[:])
             res_bf = keep.tile([P, CHUNK * PACK], BF16, name=f"res_bf{ci}", align_bytes=64)
             nc.vector.tensor_copy(
-                out=res_bf[:].rearrange("p (c i t) -> p c t i", i=2, t=PACK),
-                in_=res[:].rearrange("p t (c i) -> p c t i", i=2),
+                out=res_bf[:].rearrange("p (c i t) -> p c t i", i=PAIR, t=PACK),
+                in_=res[:].rearrange("p t (c i) -> p c t i", i=PAIR),
             )
             nc.vector.quantize_mx(out=out_codes[:, cols].bitcast(FP8X4), scales=out_scales[:, cols], in_=res_bf[:])
-            nc.sync.dma_start(out=out_words[:, cols], in_=out_codes[:, cols].bitcast(I32))
+            if ci % 2 == 1:
+                both = slice((ci - 1) * CHUNK, (ci + 1) * CHUNK)
+                nc.sync.dma_start(out=out_words[:, both], in_=out_codes[:, both].bitcast(I32))
 
-        accs = second_product(0) + second_product(1)
-        for ci in range(4):
+        accs = last_product(0) + last_product(1)
+        for ci in range(CHUNKS):
             hand_out(ci, accs[ci])
 
-        for r in range(4):
+        for r in range(SCALE_ROWS):
             queue = nc.sync if r % 2 == 0 else nc.scalar
             queue.dma_start(
-                out=out_2[0].rearrange("(q r) c -> r q c", r=4)[r].bitcast(I32), in_=out_scales[r:P:32, :].bitcast(I32)
+                out=out_2[0].rearrange("(q r) c -> r q c", r=SCALE_ROWS)[r].bitcast(I32),
+                in_=out_scales[r:P:32, :].bitcast(I32),
             )

from contextlib import ExitStack

import concourse.mybir as mybir

K, T, S, H, N = 1024, 2048, 512, 512, 512
FLOPS = 2 * K * S * H * 2 + 2 * H * S * N

F32 = mybir.dt.float32
BF16 = mybir.dt.bfloat16
I32 = mybir.dt.int32
U32 = mybir.dt.uint32
U16 = mybir.dt.uint16
U8 = mybir.dt.uint8
FP8X4 = mybir.dt.float8_e4m3fn_x4
FP4X4 = mybir.dt.float4_e2m1fn_x4
ALU = mybir.AluOpType
ACT = mybir.ActivationFunctionType

P = 128
PACK = 4
PASSES = K // (P * PACK)
SCALE_ROWS = 4
LIST_ROWS = 16
HALF = S // 2
CHUNK = 128
CHUNKS = S // CHUNK
PAIR = 2


def tile_picked_ycallgr_max_po_kernel(
    tc, x_words, x_scales, w1_words, w1_scales, w2_words, w2_scales, unit, w3_words, w3_scales, offs, cle,
    out_0, out_1, out_2,
):
    nc = tc.nc
    with ExitStack() as ctx:
        lists = ctx.enter_context(tc.tile_pool(name="lists", bufs=1))
        keep = ctx.enter_context(tc.tile_pool(name="keep", bufs=1))
        ring = ctx.enter_context(tc.tile_pool(name="ring", bufs=2))
        psum = ctx.enter_context(tc.psum_pool(name="psum", bufs=1))

        offs_sb = lists.tile([P, S // LIST_ROWS], U16, name="offs_sb")
        cle_sb = lists.tile([P, S // LIST_ROWS], U16, name="cle_sb")
        x_tab = [keep.tile([P, T], I32, name=f"x_tab{o}") for o in range(PASSES)]
        xs_tab = keep.tile([P, PASSES, T], U8, name="xs_tab")
        ws_raw = keep.tile([P, 2 * PASSES + 1, H], U8, name="ws_raw")
        w2s_raw = ws_raw[:, 0:PASSES, :]
        w1s_raw = ws_raw[:, PASSES : 2 * PASSES, :]
        w3s_raw = ws_raw[:, 2 * PASSES : 2 * PASSES + 1, :]
        unit_sb = keep.tile([P, PACK], F32, name="unit_sb")

        def load_scale_rows(queue, tile, scales, rows=range(SCALE_ROWS)):
            for r in rows:
                queue.dma_start(
                    out=tile[r:P:32, :, :].bitcast(I32),
                    in_=scales.rearrange("o (q r) c -> r q o c", r=SCALE_ROWS)[r].bitcast(I32),
                )

        def load_words(name, words):
            raw = keep.tile([P, words.shape[0], 2 * H], U8, name=name)
            nc.sync.dma_start(out=raw[:].bitcast(I32), in_=words.rearrange("o p c -> p o c").bitcast(I32))
            return raw

        def deal_words_on_scalar(name, w_raw):
            passes = w_raw.shape[1]
            dealt = keep.tile([P, passes, PACK, 2 * P], U8, name=name, align_bytes=64)
            for o in range(passes):
                nc.scalar.copy(
                    out=dealt[:, o].bitcast(U16),
                    in_=w_raw[:, o, :].bitcast(U16).rearrange("p (m t) -> p t m", t=PACK),
                )
            return dealt

        def deal_words_on_vector(name, w_raw):
            passes = w_raw.shape[1]
            dealt = keep.tile([P, passes, PACK, 2 * P], U8, name=name, align_bytes=64)
            for o in reversed(range(passes)):
                nc.vector.tensor_copy(
                    out=dealt[:, o].rearrange("p t (m b) -> p t m b", b=2),
                    in_=w_raw[:, o, :].rearrange("p (m t b) -> p t m b", t=PACK, b=2),
                )
            return dealt

        def deal_scales(name, raw):
            passes = raw.shape[1]
            dealt = keep.tile([P, passes, PACK, P], U8, name=name, align_bytes=64)
            nc.vector.tensor_copy(out=dealt[:], in_=raw.rearrange("p o (m t) -> p o t m", t=PACK))
            return dealt

        nc.gpsimd.memset(xs_tab[:, 0, :].bitcast(I32), 0)
        nc.vector.memset(xs_tab[:, 1, :].bitcast(I32), 0)
        nc.vector.memset(ws_raw[:].rearrange("p o c -> p (o c)").bitcast(I32), 0)

        nc.sync.dma_start(offs_sb[:], offs)
        w2_raw = load_words("w2_raw", w2_words)
        w3_raw = load_words("w3_raw", w3_words)
        load_scale_rows(nc.sync, xs_tab, x_scales)
        nc.sync.dma_start(out=x_tab[0][:], in_=x_words[0].rearrange("p c r -> p (c r)").bitcast(I32))
        load_scale_rows(nc.sync, w2s_raw, w2_scales)
        load_scale_rows(nc.sync, w1s_raw, w1_scales, (0, 1))
        nc.sync.dma_start(out=x_tab[1][:], in_=x_words[1].rearrange("p c r -> p (c r)").bitcast(I32))
        w1_raw = load_words("w1_raw", w1_words)
        nc.sync.dma_start(cle_sb[:], cle)
        load_scale_rows(nc.gpsimd, w1s_raw, w1_scales, (2, 3))
        nc.gpsimd.dma_start(out=unit_sb[:], in_=unit.rearrange("(p t) one -> p (t one)", t=PACK))
        load_scale_rows(nc.sync, w3s_raw, w3_scales)

        xg = [keep.tile([P, S], U32, name=f"xg{o}", align_bytes=64) for o in range(PASSES)]
        xgs = [keep.tile([P, S], U8, name=f"xgs{o}", align_bytes=64) for o in range(PASSES)]

        w2d = deal_words_on_scalar("w2d", w2_raw)
        for o in range(PASSES):
            nc.vector.tensor_copy(out=xgs[o][:], in_=xs_tab[:, o, :].indirect(offs_sb[:]))
        nc.vector.tensor_copy(out=xg[0][:], in_=x_tab[0][:].bitcast(U32).indirect(offs_sb[:]))
        w2s = deal_scales("w2s", w2s_raw)
        w1s = deal_scales("w1s", w1s_raw)
        nc.vector.tensor_copy(out=xg[1][:], in_=x_tab[1][:].bitcast(U32).indirect(offs_sb[:]))

        w1d = deal_words_on_vector("w1d", w1_raw)
        w3d = deal_words_on_scalar("w3d", w3_raw)

        sign_bf = keep.tile([P, PACK], BF16, name="sign_bf")
        unit_abs = keep.tile([P, PACK], F32, name="unit_abs")
        nc.scalar.activation(unit_abs[:], unit_sb[:], ACT.Abs)
        nc.scalar.activation(sign_bf[:], unit_sb[:], ACT.Sign)

        z_ps = [psum.tile([P, S], F32, name=f"bank_z{t}") for t in range(PACK)]
        y_ps = [psum.tile([P, S], F32, name=f"bank_y{t}") for t in range(PACK)]

        def one_pass(bank, words, scales, t, o, first):
            nc.tensor.matmul_mx(
                out=bank[:],
                lhsT=words[:, o, t, :].bitcast(FP4X4),
                lhsT_scale=scales[:, o, t, :],
                rhs=xg[o][:].bitcast(FP8X4),
                rhs_scale=xgs[o][:],
                start=(o == first),
                stop=(o != first),
            )

        for o in range(PASSES):
            for t in range(PACK):
                one_pass(z_ps[t], w2d, w2s, t, o, first=0)
        for t in range(PACK):
            for o in reversed(range(PASSES)):
                one_pass(y_ps[t], w1d, w1s, t, o, first=PASSES - 1)

        prod = keep.tile([P, PACK, S], F32, name="prod")
        z_sb = [keep.tile([P, S], F32, name=f"z_sb{t}", align_bytes=64) for t in range(PACK)]
        zc = [keep.tile([P, S], F32, name=f"zc{t}", align_bytes=64) for t in range(PACK)]

        def gather_half(on_vector, out, window, half):
            picked = window.indirect(cle_sb[:, half * HALF // LIST_ROWS : (half + 1) * HALF // LIST_ROWS])
            if on_vector:
                nc.vector.tensor_copy(out=out, in_=picked)
            else:
                nc.scalar.activation(out, picked, ACT.Copy)

        for t in range(PACK):
            nc.scalar.copy(out=z_sb[t][:], in_=z_ps[t][:])
        for t in range(PACK):
            for half in range(2):
                gather_half(t % 2 == 0, zc[t][:, half * HALF : (half + 1) * HALF], z_sb[t][:], half)
        for t in range(PACK):
            nc.vector.scalar_tensor_tensor(
                prod[:, t, :], y_ps[t][:], unit_abs[:, t : t + 1], zc[t][:], op0=ALU.mult, op1=ALU.mult
            )

        w3s = deal_scales("zc2", w3s_raw)
        out_codes = keep.tile([P, S], U32, name="out_codes", align_bytes=64)
        out_scales = keep.tile([P, S], U8, name="out_scales", align_bytes=64)
        out_rows = out_0.rearrange("(p t) c -> p t c", t=PACK)
        out_words = out_1[0].rearrange("p c r -> p (c r)").bitcast(I32)

        def last_product(half):
            callee = keep.tile([P, PACK, HALF], F32, name=("z_sb3", "zc3")[half], align_bytes=64)
            for t in range(PACK):
                gather_half(t == 0 and half == 1, callee[:, t, :], prod[:, t, :], half)
            per_half = HALF // CHUNK
            chunks = range(per_half * half, per_half * (half + 1))
            hid = {ci: ring.tile([P, CHUNK * PACK], BF16, name="hid", align_bytes=64) for ci in chunks}
            for ci in chunks:
                in_half = ci % per_half * CHUNK
                nc.vector.tensor_tensor(
                    hid[ci][:].rearrange("p (c i t) -> p c t i", i=PAIR, t=PACK),
                    prod[:, :, ci * CHUNK : (ci + 1) * CHUNK].rearrange("p t (c i) -> p c t i", i=PAIR),
                    callee[:, :, in_half : in_half + CHUNK].rearrange("p t (c i) -> p c t i", i=PAIR),
                    ALU.max,
                )
            for ci in chunks:
                nc.vector.tensor_tensor(
                    hid[ci][:].rearrange("p (j t) -> p j t", t=PACK),
                    hid[ci][:].rearrange("p (j t) -> p j t", t=PACK),
                    sign_bf[:].unsqueeze(1).to_broadcast([P, CHUNK, PACK]),
                    ALU.mult,
                )
            accs = []
            for ci in chunks:
                hq = keep.tile([P, CHUNK], U32, name=f"hq{ci}", align_bytes=64)
                hs = keep.tile([P, CHUNK], U8, name=f"hs{ci}", align_bytes=64)
                nc.vector.quantize_mx(out=hq[:].bitcast(FP8X4), scales=hs[:], in_=hid[ci][:])
                names = [f"bank_z{ci}"] if ci < CHUNKS - 1 else [f"bank_z{ci}", "bank_y0"]
                per_bank = PACK // len(names)
                acc = [psum.tile([P, per_bank, CHUNK], F32, name=name) for name in names]
                for t in range(PACK):
                    nc.tensor.matmul_mx(
                        out=acc[t // per_bank][:, t % per_bank, :],
                        lhsT=w3d[:, 0, t, :].bitcast(FP4X4),
                        lhsT_scale=w3s[:, 0, t, :],
                        rhs=hq[:].bitcast(FP8X4),
                        rhs_scale=hs[:],
                        start=True,
                        stop=True,
                    )
                accs.append(acc)
            return accs

        def hand_out(ci, acc):
            cols = slice(ci * CHUNK, (ci + 1) * CHUNK)
            res = keep.tile([P, PACK, CHUNK], F32, name=f"res{ci}")
            if len(acc) == 1:
                nc.scalar.copy(out=res[:], in_=acc[0][:])
            else:
                nc.vector.tensor_copy(out=res[:, 0 : PACK // 2, :], in_=acc[0][:])
                nc.scalar.copy(out=res[:, PACK // 2 : PACK, :], in_=acc[1][:])
            nc.sync.dma_start(out=out_rows[:, :, cols], in_=res[:])
            res_bf = keep.tile([P, CHUNK * PACK], BF16, name=f"res_bf{ci}", align_bytes=64)
            nc.vector.tensor_copy(
                out=res_bf[:].rearrange("p (c i t) -> p c t i", i=PAIR, t=PACK),
                in_=res[:].rearrange("p t (c i) -> p c t i", i=PAIR),
            )
            nc.vector.quantize_mx(out=out_codes[:, cols].bitcast(FP8X4), scales=out_scales[:, cols], in_=res_bf[:])
            if ci % 2 == 1:
                both = slice((ci - 1) * CHUNK, (ci + 1) * CHUNK)
                nc.sync.dma_start(out=out_words[:, both], in_=out_codes[:, both].bitcast(I32))

        accs = last_product(0) + last_product(1)
        for ci in range(CHUNKS):
            hand_out(ci, accs[ci])

        for r in range(SCALE_ROWS):
            queue = nc.sync if r % 2 == 0 else nc.scalar
            queue.dma_start(
                out=out_2[0].rearrange("(q r) c -> r q c", r=SCALE_ROWS)[r].bitcast(I32),
                in_=out_scales[r:P:32, :].bitcast(I32),
            )
